import numpy as np
import ml_dtypes


def mxq(x, axis, fmt="e4m3"):
    dtype, down = {"e4m3": (ml_dtypes.float8_e4m3fn, 7), "e5m2": (ml_dtypes.float8_e5m2, 14)}[fmt]
    v = np.moveaxis(np.asarray(x, np.float32).astype(ml_dtypes.bfloat16).astype(np.float64), axis, -1)
    blocks = v.reshape(v.shape[:-1] + (-1, 32))
    amax = np.abs(blocks).max(-1, keepdims=True)
    byte = np.maximum(np.where(amax > 0, np.frexp(amax)[1] - 1 + 127, 0) - down, 1)
    scale = np.exp2(byte - 127.0)
    codes = (blocks / scale).astype(np.float32).astype(dtype).astype(np.float64)
    return np.moveaxis((codes * scale).reshape(v.shape), -1, axis)


WIDE = False


def mx_kscale(k):
    if not WIDE:
        return np.ones(k)
    levels = np.array([10, -10, 5, -5, 0])
    if k % 512:
        return np.exp2(np.random.permutation(np.resize(levels, k // 32))).repeat(32)
    a = np.empty((k // 512, 16))
    for p in range(k // 512):
        a[p, :8] = np.random.permutation(np.resize(levels, 8))
        for g in range(8):
            far = levels[np.abs(levels - a[p, g]) >= 10]
            a[p, g + 8] = far[np.random.randint(len(far))]
    return np.exp2(a.ravel()).repeat(32)


def f64(x):
    return np.asarray(x).astype(np.float64)


def striped(idx):
    return np.tile(idx.reshape(-1, 16).T, (8, 1)).astype(np.uint16)


def unstriped(offs):
    return offs[:16].T.reshape(-1).astype(np.int64)


K, T, E, C, N = 128, 1024, 8, 128, 1536


def by_expert(wq, xq):
    return np.concatenate([wq[e].T @ xq[:, e * C:(e + 1) * C] for e in range(E)], axis=1)


def setup_inputs():
    n = np.random.standard_normal
    s = mx_kscale(N)[:, None]
    return {
        "dyT": (n((N, T)) * s).astype(np.float32),
        "w": (n((E, N, K)) / np.sqrt(N) / s[None]).astype(np.float32),
        "gate": np.tile(np.random.uniform(0.2, 1.0, E * C), (N, 1)).astype(np.float32),
        "offs": striped(np.random.permutation(T)[:E * C]),
    }


def reference(dyT, w, gate, offs):
    idx = unstriped(offs)
    gq = mxq(f64(gate) * f64(dyT)[:, idx], 0, "e4m3")
    dx = by_expert(mxq(f64(w), 1, "e4m3"), gq)
    out = np.zeros((K, T))
    out[:, idx] = dx
    return out

@@ -1,0 +1,207 @@
+from contextlib import ExitStack
+
+import concourse.mybir as mybir
+
+F32 = mybir.dt.float32
+BF16 = mybir.dt.bfloat16
+U32 = mybir.dt.uint32
+U16 = mybir.dt.uint16
+U8 = mybir.dt.uint8
+FP8X4 = mybir.dt.float8_e4m3fn_x4
+MULT = mybir.AluOpType.mult
+
+K, T, E, C, N = 128, 1024, 8, 128, 1536
+S = E * C
+P = 128
+PACK = 4
+K_PASS = P * PACK
+PASSES = N // K_PASS
+PAD = 32
+HALF = E // 2
+
+FLOPS = 2 * K * N * S
+BYTES = 4 * (N * T + E * N * K + K * T + S) + 2 * S
+
+
+def tile_moe_bdx_lin_none_kernel(tc, dyT, w, gate, offs, out):
+    nc = tc.nc
+    with ExitStack() as ctx:
+        keep = ctx.enter_context(tc.tile_pool(name="keep", bufs=1))
+        stage = ctx.enter_context(tc.tile_pool(name="stage", bufs=2))
+        psum = ctx.enter_context(tc.psum_pool(name="psum", bufs=1))
+
+        offsets = keep.tile([P, S // 16], U16, name="offsets")
+        gates = keep.tile([P, S], F32, name="gates")
+        windows = {}
+        w_raw = {}
+        for c in range(PASSES):
+            for t in range(PACK):
+                width = T + PAD if c < 2 else T
+                windows[c, t] = keep.tile([P, width], F32, name=f"win{c}{t}")
+                if c < 2:
+                    nc.gpsimd.memset(windows[c, t][:, T:width], 0.0)
+            for h in range(4):
+                w_raw[c, h] = keep.tile([P, 2, PACK, K], F32, name=f"wraw{c}{h}")
+        g_codes = keep.tile([P, PASSES, S], U32, align_bytes=64, name="g_codes")
+        g_scales = keep.tile([P, PASSES, S], U8, align_bytes=64, name="g_scales")
+        w_codes = keep.tile([P, PASSES, E * K], U32, align_bytes=64, name="w_codes")
+        w_scales = keep.tile([P, PASSES, E * K], U8, align_bytes=64, name="w_scales")
+        result = keep.tile([P, T], F32, name="result")
+        slots = keep.tile([P, S], F32, name="slots")
+        acc = [psum.tile([P, C], F32, name=f"acc{e}") for e in range(E)]
+
+        dy_rows = dyT.rearrange("(c p j) t -> c p j t", p=P, j=PACK)
+        w_rows = w.rearrange("e (c p j) k -> c p e (j k)", p=P, j=PACK)
+
+        def load_window(c, t):
+            nc.sync.dma_start(out=windows[c, t][:, 0:T], in_=dy_rows[c, :, t, :])
+
+        def load_w(c, h):
+            nc.sync.dma_start(
+                out=w_raw[c, h][:].rearrange("p e j k -> p e (j k)"),
+                in_=w_rows[c, :, 2 * h : 2 * h + 2, :],
+            )
+
+        nc.sync.dma_start(offsets[:], offs)
+        load_window(0, 0)
+        nc.sync.dma_start(out=gates[:, 0:256], in_=gate[0:P, 0:256])
+        nc.sync.dma_start(out=gates[:, 256:1024], in_=gate[0:P, 256:1024])
+        wins = [(c, t) for c in range(PASSES) for t in range(PACK)]
+        ws = [(c, h) for c in range(PASSES) for h in range(4)]
+        for i in range(11):
+            load_window(*wins[i + 1])
+            load_w(*ws[i])
+        load_w(*ws[11])
+
+        gathered = {}
+
+        def gather(c, s0, n, t):
+            q = s0 // 512
+            if (c, q) not in gathered:
+                gathered[c, q] = stage.tile([P, PACK, 1024 if c < 2 else 512], F32, tag=f"gathered{c < 2}", name=f"gathered{c}{q}")
+            base = 0 if c < 2 else q * 512
+            nc.vector.tensor_tensor(
+                gathered[c, q][:, t, s0 - base : s0 - base + n],
+                windows[c, t][:].indirect(offsets[:, s0 // 16 : (s0 + n) // 16]),
+                gates[:, s0 : s0 + n],
+                MULT,
+            )
+            if n == 768:
+                gathered[c, 0] = gathered[c, q]
+
+        mixed = {}
+
+        def mix_g(c, q, s0, n, base, width):
+            if s0 == base:
+                mixed[c, q] = stage.tile([P, width, PACK], BF16, align_bytes=64, tag=f"gmix{width}", name=f"gmix{c}{q}")
+            nc.scalar.copy(
+                out=mixed[c, q][:, s0 - base : s0 - base + n, :],
+                in_=gathered[c, q][:, :, s0 - base : s0 - base + n].rearrange("p t n -> p n t"),
+            )
+
+        def quant_g(c, q, s0, n):
+            nc.vector.quantize_mx(
+                out=g_codes[:, c, s0 : s0 + n].bitcast(FP8X4),
+                scales=g_scales[:, c, s0 : s0 + n],
+                in_=mixed[c, q][:].rearrange("p n t -> p (n t)"),
+            )
+
+        wmixed = {}
+
+        def mix_w(c, h):
+            if h % 2 == 0:
+                wmixed[c, h // 2] = stage.tile([P, HALF, K, PACK], BF16, align_bytes=64, tag="wmix", name=f"wmix{c}{h}")
+            e0 = 2 * (h % 2)
+            nc.scalar.copy(
+                out=wmixed[c, h // 2][:, e0 : e0 + 2],
+                in_=w_raw[c, h][:].rearrange("p e j k -> p e k j"),
+            )
+
+        def quant_w(c, q):
+            k0 = q * HALF * K
+            n = HALF * K
+            nc.vector.quantize_mx(
+                out=w_codes[:, c, k0 : k0 + n].bitcast(FP8X4),
+                scales=w_scales[:, c, k0 : k0 + n],
+                in_=wmixed[c, q][:].rearrange("p e k j -> p (e k j)"),
+            )
+
+        def multiply(c, e0, e1):
+            for e in range(e0, e1):
+                cols = slice(e * C, (e + 1) * C)
+                nc.tensor.matmul_mx(
+                    out=acc[e][:],
+                    lhsT=w_codes[:, c, cols].bitcast(FP8X4),
+                    lhsT_scale=w_scales[:, c, cols],
+                    rhs=g_codes[:, c, cols].bitcast(FP8X4),
+                    rhs_scale=g_scales[:, c, cols],
+                    start=(c == 0),
+                    stop=(c == PASSES - 1),
+                )
+
+        def drain(e0, e1):
+            for e in range(e0, e1):
+                nc.scalar.copy(out=slots[:, e * C : (e + 1) * C], in_=acc[e][:])
+
+        def scatter(s0, n):
+            nc.vector.tensor_copy(
+                out=result[:].indirect(offsets[:, s0 // 16 : (s0 + n) // 16]), in_=slots[:, s0 : s0 + n]
+            )
+
+        gather(0, 0, 256, 0)
+        q0 = gathered[0, 0]
+        nc.vector.tensor_tensor(q0[:, 0, 256:1024], windows[0, 0][:].indirect(offsets[:, 16:64]), gates[:, 256:1024], MULT)
+        mix_w(0, 0)
+        gather(0, 0, 1024, 1)
+        mix_w(0, 1)
+        gather(0, 0, 1024, 2)
+        quant_w(0, 0)
+        mix_w(0, 2)
+        gather(0, 0, 1024, 3)
+        mix_g(0, 0, 0, 512, 0, 1024)
+        mix_g(0, 0, 512, 512, 0, 1024)
+        mix_w(0, 3)
+        gather(1, 0, 1024, 0)
+        gather(1, 0, 1024, 1)
+        mix_w(1, 0)
+        gather(1, 0, 1024, 2)
+        quant_g(0, 0, 0, 1024)
+        quant_w(0, 1)
+        multiply(0, 0, 8)
+        mix_w(1, 1)
+        mix_w(1, 2)
+        mix_w(1, 3)
+        gather(1, 0, 1024, 3)
+        mix_g(1, 0, 0, 512, 0, 1024)
+        mix_g(1, 0, 512, 512, 0, 1024)
+        gather(2, 0, 512, 0)
+        quant_w(1, 0)
+        gather(2, 0, 512, 1)
+        quant_w(1, 1)
+        mix_w(2, 0)
+        mix_w(2, 1)
+        gather(2, 0, 512, 2)
+        gather(2, 0, 512, 3)
+        mix_g(2, 0, 0, 512, 0, 512)
+        gather(2, 512, 512, 0)
+        quant_g(1, 0, 0, 1024)
+        multiply(1, 0, 8)
+        gather(2, 512, 512, 1)
+        quant_w(2, 0)
+        gather(2, 512, 512, 2)
+        quant_g(2, 0, 0, 512)
+        multiply(2, 0, 4)
+        drain(0, 4)
+        mix_w(2, 2)
+        mix_w(2, 3)
+        gather(2, 512, 512, 3)
+        mix_g(2, 1, 512, 512, 512, 512)
+        quant_w(2, 1)
+        scatter(0, 384)
+        quant_g(2, 1, 512, 512)
+        multiply(2, 4, 8)
+        drain(4, 8)
+        scatter(384, 128)
+        scatter(512, 256)
+        scatter(768, 256)
+        nc.sync.dma_start(out=out, in_=result[:])

@@ -17,7 +17,7 @@ PACK = 4
 K_PASS = P * PACK
 PASSES = N // K_PASS
 PAD = 32
-HALF = E // 2
+RUN = 4
 
 FLOPS = 2 * K * N * S
 BYTES = 4 * (N * T + E * N * K + K * T + S) + 2 * S
@@ -36,9 +36,9 @@ def tile_moe_bdx_lin_none_kernel(tc, dyT, w, gate, offs, out):
         w_raw = {}
         for c in range(PASSES):
             for t in range(PACK):
-                width = T + PAD if c < 2 else T
+                width = T + PAD if c == 1 else T
                 windows[c, t] = keep.tile([P, width], F32, name=f"win{c}{t}")
-                if c < 2:
+                if c == 1:
                     nc.gpsimd.memset(windows[c, t][:, T:width], 0.0)
             for h in range(4):
                 w_raw[c, h] = keep.tile([P, 2, PACK, K], F32, name=f"wraw{c}{h}")
@@ -62,41 +62,31 @@ def tile_moe_bdx_lin_none_kernel(tc, dyT, w, gate, offs, out):
                 in_=w_rows[c, :, 2 * h : 2 * h + 2, :],
             )
 
-        nc.sync.dma_start(offsets[:], offs)
-        load_window(0, 0)
-        nc.sync.dma_start(out=gates[:, 0:256], in_=gate[0:P, 0:256])
-        nc.sync.dma_start(out=gates[:, 256:1024], in_=gate[0:P, 256:1024])
-        wins = [(c, t) for c in range(PASSES) for t in range(PACK)]
-        ws = [(c, h) for c in range(PASSES) for h in range(4)]
-        for i in range(11):
-            load_window(*wins[i + 1])
-            load_w(*ws[i])
-        load_w(*ws[11])
+        def load_gates(s0, s1):
+            nc.sync.dma_start(out=gates[:, s0:s1], in_=gate[0:P, s0:s1])
 
         gathered = {}
 
-        def gather(c, s0, n, t):
-            q = s0 // 512
-            if (c, q) not in gathered:
-                gathered[c, q] = stage.tile([P, PACK, 1024 if c < 2 else 512], F32, tag=f"gathered{c < 2}", name=f"gathered{c}{q}")
-            base = 0 if c < 2 else q * 512
+        def new_gathered(c, q, n):
+            gathered[c, q] = stage.tile([P, PACK, n], F32, tag=f"gathered{n}", bufs=1 if n == 1024 else 3, name=f"gathered{c}{q}")
+
+        def gather(c, q, t, s0, n):
             nc.vector.tensor_tensor(
-                gathered[c, q][:, t, s0 - base : s0 - base + n],
+                gathered[c, q][:, t, :],
                 windows[c, t][:].indirect(offsets[:, s0 // 16 : (s0 + n) // 16]),
                 gates[:, s0 : s0 + n],
                 MULT,
             )
-            if n == 768:
-                gathered[c, 0] = gathered[c, q]
 
         mixed = {}
 
-        def mix_g(c, q, s0, n, base, width):
-            if s0 == base:
-                mixed[c, q] = stage.tile([P, width, PACK], BF16, align_bytes=64, tag=f"gmix{width}", name=f"gmix{c}{q}")
+        def new_mixed(c, q, n):
+            mixed[c, q] = stage.tile([P, n, PACK], BF16, align_bytes=64, tag=f"mixed{n}", bufs=1 if n == 1024 else 2, name=f"mixed{c}{q}")
+
+        def mix(dst, src):
             nc.scalar.copy(
-                out=mixed[c, q][:, s0 - base : s0 - base + n, :],
-                in_=gathered[c, q][:, :, s0 - base : s0 - base + n].rearrange("p t n -> p n t"),
+                out=dst.rearrange("p (n i) t -> p n t i", i=RUN),
+                in_=src.rearrange("p t (n i) -> p n t i", i=RUN),
             )
 
         def quant_g(c, q, s0, n):
@@ -110,19 +100,18 @@ def tile_moe_bdx_lin_none_kernel(tc, dyT, w, gate, offs, out):
 
         def mix_w(c, h):
             if h % 2 == 0:
-                wmixed[c, h // 2] = stage.tile([P, HALF, K, PACK], BF16, align_bytes=64, tag="wmix", name=f"wmix{c}{h}")
+                wmixed[c, h // 2] = stage.tile([P, 4, K, PACK], BF16, align_bytes=64, tag="wmix", bufs=2, name=f"wmix{c}{h}")
             e0 = 2 * (h % 2)
             nc.scalar.copy(
-                out=wmixed[c, h // 2][:, e0 : e0 + 2],
-                in_=w_raw[c, h][:].rearrange("p e j k -> p e k j"),
+                out=wmixed[c, h // 2][:, e0 : e0 + 2].rearrange("p e (k i) j -> p e k j i", i=RUN),
+                in_=w_raw[c, h][:].rearrange("p e j (k i) -> p e k j i", i=RUN),
             )
 
         def quant_w(c, q):
-            k0 = q * HALF * K
-            n = HALF * K
+            cols = slice(q * 4 * K, (q + 1) * 4 * K)
             nc.vector.quantize_mx(
-                out=w_codes[:, c, k0 : k0 + n].bitcast(FP8X4),
-                scales=w_scales[:, c, k0 : k0 + n],
+                out=w_codes[:, c, cols].bitcast(FP8X4),
+                scales=w_scales[:, c, cols],
                 in_=wmixed[c, q][:].rearrange("p e k j -> p (e k j)"),
             )
 
@@ -138,69 +127,98 @@ def tile_moe_bdx_lin_none_kernel(tc, dyT, w, gate, offs, out):
                     start=(c == 0),
                     stop=(c == PASSES - 1),
                 )
-
-        def drain(e0, e1):
-            for e in range(e0, e1):
-                nc.scalar.copy(out=slots[:, e * C : (e + 1) * C], in_=acc[e][:])
+                if c == PASSES - 1:
+                    nc.scalar.copy(out=slots[:, cols], in_=acc[e][:])
 
         def scatter(s0, n):
             nc.vector.tensor_copy(
                 out=result[:].indirect(offsets[:, s0 // 16 : (s0 + n) // 16]), in_=slots[:, s0 : s0 + n]
             )
 
-        gather(0, 0, 256, 0)
-        q0 = gathered[0, 0]
-        nc.vector.tensor_tensor(q0[:, 0, 256:1024], windows[0, 0][:].indirect(offsets[:, 16:64]), gates[:, 256:1024], MULT)
+        nc.sync.dma_start(offsets[:], offs)
+        load_window(0, 0)
+        load_gates(0, 512)
+        load_window(0, 1)
+        load_window(0, 2)
+        load_window(0, 3)
+        load_gates(512, 1024)
+        load_w(0, 0)
+        load_w(0, 1)
+        load_w(0, 2)
+        ws = [(0, 3), (1, 0), (1, 1), (1, 2), (1, 3), (2, 0), (2, 1), (2, 2)]
+        for i in range(8):
+            load_window(1 + i // 4, i % 4)
+            load_w(*ws[i])
+        load_w(2, 3)
+
+        new_gathered(0, 0, 512)
+        new_gathered(0, 1, 512)
+        for t in range(4):
+            gather(0, 0, t, 0, 512)
+        new_mixed(0, 0, 512)
+        mix(mixed[0, 0][:], gathered[0, 0][:])
         mix_w(0, 0)
-        gather(0, 0, 1024, 1)
         mix_w(0, 1)
-        gather(0, 0, 1024, 2)
-        quant_w(0, 0)
+        gather(0, 1, 0, 512, 512)
+        gather(0, 1, 1, 512, 512)
+        gather(0, 1, 2, 512, 512)
+        quant_g(0, 0, 0, 512)
+        gather(0, 1, 3, 512, 512)
+        new_mixed(0, 1, 512)
+        mix(mixed[0, 1][:], gathered[0, 1][:])
         mix_w(0, 2)
-        gather(0, 0, 1024, 3)
-        mix_g(0, 0, 0, 512, 0, 1024)
-        mix_g(0, 0, 512, 512, 0, 1024)
         mix_w(0, 3)
-        gather(1, 0, 1024, 0)
-        gather(1, 0, 1024, 1)
+        new_gathered(1, 0, 1024)
+        gather(1, 0, 0, 0, 1024)
+        quant_w(0, 0)
+        multiply(0, 0, 4)
         mix_w(1, 0)
-        gather(1, 0, 1024, 2)
-        quant_g(0, 0, 0, 1024)
-        quant_w(0, 1)
-        multiply(0, 0, 8)
+        gather(1, 0, 1, 0, 1024)
+        quant_g(0, 1, 512, 512)
         mix_w(1, 1)
+        gather(1, 0, 2, 0, 1024)
+        quant_w(0, 1)
+        multiply(0, 4, 8)
         mix_w(1, 2)
         mix_w(1, 3)
-        gather(1, 0, 1024, 3)
-        mix_g(1, 0, 0, 512, 0, 1024)
-        mix_g(1, 0, 512, 512, 0, 1024)
-        gather(2, 0, 512, 0)
+        gather(1, 0, 3, 0, 1024)
+        new_mixed(1, 0, 1024)
+        mix(mixed[1, 0][:, 0:512], gathered[1, 0][:, :, 0:512])
+        mix(mixed[1, 0][:, 512:1024], gathered[1, 0][:, :, 512:1024])
+        new_gathered(2, 0, 512)
+        new_gathered(2, 1, 512)
+        gather(2, 0, 0, 0, 512)
         quant_w(1, 0)
-        gather(2, 0, 512, 1)
-        quant_w(1, 1)
+        gather(2, 0, 1, 0, 512)
         mix_w(2, 0)
         mix_w(2, 1)
-        gather(2, 0, 512, 2)
-        gather(2, 0, 512, 3)
-        mix_g(2, 0, 0, 512, 0, 512)
-        gather(2, 512, 512, 0)
+        quant_w(1, 1)
+        gather(2, 0, 2, 0, 512)
+        gather(2, 0, 3, 0, 512)
+        new_mixed(2, 0, 512)
+        mix(mixed[2, 0][:], gathered[2, 0][:])
+        gather(2, 1, 0, 512, 512)
         quant_g(1, 0, 0, 1024)
         multiply(1, 0, 8)
-        gather(2, 512, 512, 1)
+        gather(2, 1, 1, 512, 512)
         quant_w(2, 0)
-        gather(2, 512, 512, 2)
-        quant_g(2, 0, 0, 512)
-        multiply(2, 0, 4)
-        drain(0, 4)
         mix_w(2, 2)
         mix_w(2, 3)
-        gather(2, 512, 512, 3)
-        mix_g(2, 1, 512, 512, 512, 512)
+        gather(2, 1, 2, 512, 512)
+        quant_g(2, 0, 0, 512)
+        multiply(2, 0, 4)
+        gather(2, 1, 3, 512, 512)
+        new_mixed(2, 1, 256)
+        mix(mixed[2, 1][:], gathered[2, 1][:, :, 0:256])
+        new_mixed(2, 2, 256)
+        mix(mixed[2, 2][:], gathered[2, 1][:, :, 256:512])
         quant_w(2, 1)
-        scatter(0, 384)
-        quant_g(2, 1, 512, 512)
-        multiply(2, 4, 8)
-        drain(4, 8)
+        scatter(0, 256)
+        quant_g(2, 1, 512, 256)
+        multiply(2, 4, 6)
+        scatter(256, 128)
+        quant_g(2, 2, 768, 256)
+        multiply(2, 6, 8)
         scatter(384, 128)
         scatter(512, 256)
         scatter(768, 256)

@@ -18,6 +18,7 @@ K_PASS = P * PACK
 PASSES = N // K_PASS
 PAD = 32
 RUN = 4
+LOADS = [(x[0], int(x[1]), int(x[2])) for x in "w00 w01 y10 y11 y12 w02 w03 w10 w11 w12 w13 y13 w20 y20 y21 y22 y23 w21 w22 w23".split(" ")]
 
 FLOPS = 2 * K * N * S
 BYTES = 4 * (N * T + E * N * K + K * T + S) + 2 * S
@@ -40,15 +41,15 @@ def tile_moe_bdx_lin_none_kernel(tc, dyT, w, gate, offs, out):
                 windows[c, t] = keep.tile([P, width], F32, name=f"win{c}{t}")
                 if c == 1:
                     nc.gpsimd.memset(windows[c, t][:, T:width], 0.0)
-            for h in range(4):
-                w_raw[c, h] = keep.tile([P, 2, PACK, K], F32, name=f"wraw{c}{h}")
+            for h in range(2):
+                w_raw[c, h] = keep.tile([P, 4, PACK, K], F32, name=f"wraw{c}{h}")
         g_codes = keep.tile([P, PASSES, S], U32, align_bytes=64, name="g_codes")
         g_scales = keep.tile([P, PASSES, S], U8, align_bytes=64, name="g_scales")
         w_codes = keep.tile([P, PASSES, E * K], U32, align_bytes=64, name="w_codes")
         w_scales = keep.tile([P, PASSES, E * K], U8, align_bytes=64, name="w_scales")
         result = keep.tile([P, T], F32, name="result")
         slots = keep.tile([P, S], F32, name="slots")
-        acc = [psum.tile([P, C], F32, name=f"acc{e}") for e in range(E)]
+        acc = [psum.tile([P, 2 * C], F32, name=f"acc{b}") for b in range(E // 2)]
 
         dy_rows = dyT.rearrange("(c p j) t -> c p j t", p=P, j=PACK)
         w_rows = w.rearrange("e (c p j) k -> c p e (j k)", p=P, j=PACK)
@@ -58,7 +59,7 @@ def tile_moe_bdx_lin_none_kernel(tc, dyT, w, gate, offs, out):
 
         def load_w(c, h):
             nc.sync.dma_start(
-                out=w_raw[c, h][:].rearrange("p e j k -> p e (j k)"),
+                out=w_raw[c, h // 2][:, 2 * (h % 2) : 2 * (h % 2) + 2].rearrange("p e j k -> p e (j k)"),
                 in_=w_rows[c, :, 2 * h : 2 * h + 2, :],
             )
 
@@ -68,7 +69,7 @@ def tile_moe_bdx_lin_none_kernel(tc, dyT, w, gate, offs, out):
         gathered = {}
 
         def new_gathered(c, q, n):
-            gathered[c, q] = stage.tile([P, PACK, n], F32, tag=f"gathered{n}", bufs=1 if n == 1024 else 3, name=f"gathered{c}{q}")
+            gathered[c, q] = stage.tile([P, PACK, n], F32, tag="gathered_b" if (c, q) in ((1, 0), (2, 1)) else "gathered_a", bufs=1 if (c, q) in ((1, 0), (2, 1)) else 2, name=f"gathered{c}{q}")
 
         def gather(c, q, t, s0, n):
             nc.vector.tensor_tensor(
@@ -81,7 +82,7 @@ def tile_moe_bdx_lin_none_kernel(tc, dyT, w, gate, offs, out):
         mixed = {}
 
         def new_mixed(c, q, n):
-            mixed[c, q] = stage.tile([P, n, PACK], BF16, align_bytes=64, tag=f"mixed{n}", bufs=1 if n == 1024 else 2, name=f"mixed{c}{q}")
+            mixed[c, q] = stage.tile([P, n, PACK], BF16, align_bytes=64, tag=f"mixed{n}", bufs=1 if n == 1024 else 3, name=f"mixed{c}{q}")
 
         def mix(dst, src):
             nc.scalar.copy(
@@ -98,13 +99,11 @@ def tile_moe_bdx_lin_none_kernel(tc, dyT, w, gate, offs, out):
 
         wmixed = {}
 
-        def mix_w(c, h):
-            if h % 2 == 0:
-                wmixed[c, h // 2] = stage.tile([P, 4, K, PACK], BF16, align_bytes=64, tag="wmix", bufs=2, name=f"wmix{c}{h}")
-            e0 = 2 * (h % 2)
+        def mix_w(c, q):
+            wmixed[c, q] = stage.tile([P, 4, K, PACK], BF16, align_bytes=64, tag="wmix", bufs=6, name=f"wmix{c}{q}")
             nc.scalar.copy(
-                out=wmixed[c, h // 2][:, e0 : e0 + 2].rearrange("p e (k i) j -> p e k j i", i=RUN),
-                in_=w_raw[c, h][:].rearrange("p e j (k i) -> p e k j i", i=RUN),
+                out=wmixed[c, q][:].rearrange("p e (k i) j -> p e k j i", i=RUN),
+                in_=w_raw[c, q][:].rearrange("p e j (k i) -> p e k j i", i=RUN),
             )
 
         def quant_w(c, q):
@@ -115,20 +114,24 @@ def tile_moe_bdx_lin_none_kernel(tc, dyT, w, gate, offs, out):
                 in_=wmixed[c, q][:].rearrange("p e k j -> p (e k j)"),
             )
 
-        def multiply(c, e0, e1):
-            for e in range(e0, e1):
-                cols = slice(e * C, (e + 1) * C)
-                nc.tensor.matmul_mx(
-                    out=acc[e][:],
-                    lhsT=w_codes[:, c, cols].bitcast(FP8X4),
-                    lhsT_scale=w_scales[:, c, cols],
-                    rhs=g_codes[:, c, cols].bitcast(FP8X4),
-                    rhs_scale=g_scales[:, c, cols],
-                    start=(c == 0),
-                    stop=(c == PASSES - 1),
-                )
-                if c == PASSES - 1:
-                    nc.scalar.copy(out=slots[:, cols], in_=acc[e][:])
+        def multiply(c, e):
+            cols = slice(e * C, (e + 1) * C)
+            half = (e % 2) * C
+            nc.tensor.matmul_mx(
+                out=acc[e // 2][:, half : half + C],
+                lhsT=w_codes[:, c, cols].bitcast(FP8X4),
+                lhsT_scale=w_scales[:, c, cols],
+                rhs=g_codes[:, c, cols].bitcast(FP8X4),
+                rhs_scale=g_scales[:, c, cols],
+                start=(c == 0),
+                stop=(c == PASSES - 1),
+            )
+
+        def finish(b):
+            multiply(2, 2 * b)
+            for c in range(PASSES):
+                multiply(c, 2 * b + 1)
+            nc.scalar.copy(out=slots[:, 2 * b * C : 2 * (b + 1) * C], in_=acc[b][:])
 
         def scatter(s0, n):
             nc.vector.tensor_copy(
@@ -142,83 +145,98 @@ def tile_moe_bdx_lin_none_kernel(tc, dyT, w, gate, offs, out):
         load_window(0, 2)
         load_window(0, 3)
         load_gates(512, 1024)
-        load_w(0, 0)
-        load_w(0, 1)
-        load_w(0, 2)
-        ws = [(0, 3), (1, 0), (1, 1), (1, 2), (1, 3), (2, 0), (2, 1), (2, 2)]
-        for i in range(8):
-            load_window(1 + i // 4, i % 4)
-            load_w(*ws[i])
-        load_w(2, 3)
+        for kind, c, i in LOADS:
+            (load_window if kind == "y" else load_w)(c, i)
 
-        new_gathered(0, 0, 512)
-        new_gathered(0, 1, 512)
-        for t in range(4):
-            gather(0, 0, t, 0, 512)
-        new_mixed(0, 0, 512)
-        mix(mixed[0, 0][:], gathered[0, 0][:])
+        def g0(q, t):
+            if t == 0:
+                new_gathered(0, q, 512)
+            gather(0, q, t, 512 * q, 512)
+
+        def g1(t):
+            if t == 0:
+                new_gathered(1, 0, 1024)
+            gather(1, 0, t, 0, 1024)
+
+        def g2(q, t):
+            if t == 0:
+                new_gathered(2, q, 512)
+            gather(2, q, t, 512 * q, 512)
+
+        def m0(q):
+            new_mixed(0, q, 512)
+            mix(mixed[0, q][:], gathered[0, q][:])
+
+        def m1():
+            new_mixed(1, 0, 1024)
+            mix(mixed[1, 0][:], gathered[1, 0][:])
+
+        def m2a():
+            new_mixed(2, 0, 512)
+            mix(mixed[2, 0][:], gathered[2, 0][:])
+
+        def m2b(i):
+            new_mixed(2, 1 + i, 256)
+            mix(mixed[2, 1 + i][:], gathered[2, 1][:, :, 256 * i : 256 * i + 256])
+
         mix_w(0, 0)
+        g0(0, 0)
+        g0(0, 1)
+        g0(0, 2)
+        g0(0, 3)
+        g0(1, 0)
+        g0(1, 1)
         mix_w(0, 1)
-        gather(0, 1, 0, 512, 512)
-        gather(0, 1, 1, 512, 512)
-        gather(0, 1, 2, 512, 512)
-        quant_g(0, 0, 0, 512)
-        gather(0, 1, 3, 512, 512)
-        new_mixed(0, 1, 512)
-        mix(mixed[0, 1][:], gathered[0, 1][:])
-        mix_w(0, 2)
-        mix_w(0, 3)
-        new_gathered(1, 0, 1024)
-        gather(1, 0, 0, 0, 1024)
-        quant_w(0, 0)
-        multiply(0, 0, 4)
+        g0(1, 2)
+        m0(0)
+        g0(1, 3)
         mix_w(1, 0)
-        gather(1, 0, 1, 0, 1024)
-        quant_g(0, 1, 512, 512)
-        mix_w(1, 1)
-        gather(1, 0, 2, 0, 1024)
+        g1(0)
         quant_w(0, 1)
-        multiply(0, 4, 8)
-        mix_w(1, 2)
-        mix_w(1, 3)
-        gather(1, 0, 3, 0, 1024)
-        new_mixed(1, 0, 1024)
-        mix(mixed[1, 0][:, 0:512], gathered[1, 0][:, :, 0:512])
-        mix(mixed[1, 0][:, 512:1024], gathered[1, 0][:, :, 512:1024])
-        new_gathered(2, 0, 512)
-        new_gathered(2, 1, 512)
-        gather(2, 0, 0, 0, 512)
-        quant_w(1, 0)
-        gather(2, 0, 1, 0, 512)
+        g1(1)
+        quant_g(0, 0, 0, 512)
+        g1(2)
+        g1(3)
+        mix_w(1, 1)
+        g2(0, 0)
+        g2(0, 1)
         mix_w(2, 0)
         mix_w(2, 1)
-        quant_w(1, 1)
-        gather(2, 0, 2, 0, 512)
-        gather(2, 0, 3, 0, 512)
-        new_mixed(2, 0, 512)
-        mix(mixed[2, 0][:], gathered[2, 0][:])
-        gather(2, 1, 0, 512, 512)
+        m1()
+        m0(1)
         quant_g(1, 0, 0, 1024)
-        multiply(1, 0, 8)
-        gather(2, 1, 1, 512, 512)
         quant_w(2, 0)
-        mix_w(2, 2)
-        mix_w(2, 3)
-        gather(2, 1, 2, 512, 512)
+        quant_g(0, 1, 512, 512)
+        multiply(0, 4)
+        multiply(0, 6)
+        g2(0, 2)
+        g2(0, 3)
+        quant_w(1, 1)
+        multiply(1, 4)
+        multiply(1, 6)
+        m2a()
+        quant_w(1, 0)
         quant_g(2, 0, 0, 512)
-        multiply(2, 0, 4)
-        gather(2, 1, 3, 512, 512)
-        new_mixed(2, 1, 256)
-        mix(mixed[2, 1][:], gathered[2, 1][:, :, 0:256])
-        new_mixed(2, 2, 256)
-        mix(mixed[2, 2][:], gathered[2, 1][:, :, 256:512])
+        quant_w(0, 0)
+        multiply(0, 0)
+        multiply(0, 2)
+        multiply(1, 0)
+        multiply(1, 2)
+        g2(1, 0)
+        finish(0)
+        g2(1, 1)
         quant_w(2, 1)
-        scatter(0, 256)
+        g2(1, 2)
+        g2(1, 3)
+        m2b(0)
+        finish(1)
         quant_g(2, 1, 512, 256)
-        multiply(2, 4, 6)
+        scatter(0, 256)
+        finish(2)
+        m2b(1)
         scatter(256, 128)
         quant_g(2, 2, 768, 256)
-        multiply(2, 6, 8)
+        finish(3)
         scatter(384, 128)
         scatter(512, 256)
         scatter(768, 256)

@@ -18,7 +18,7 @@ K_PASS = P * PACK
 PASSES = N // K_PASS
 PAD = 32
 RUN = 4
-LOADS = [(x[0], int(x[1]), int(x[2])) for x in "w00 w01 y10 y11 y12 w02 w03 w10 w11 w12 w13 y13 w20 y20 y21 y22 y23 w21 w22 w23".split(" ")]
+LOADS = [(x[0], int(x[1]), int(x[2])) for x in "y01 y02 w00 w01 y03 y10 w02 y11 w03 w10 y12 y13 w11 w12 w13 y20 y21 y22 y23 w20 w21 w22 w23".split(" ")]
 
 FLOPS = 2 * K * N * S
 BYTES = 4 * (N * T + E * N * K + K * T + S) + 2 * S
@@ -37,9 +37,9 @@ def tile_moe_bdx_lin_none_kernel(tc, dyT, w, gate, offs, out):
         w_raw = {}
         for c in range(PASSES):
             for t in range(PACK):
-                width = T + PAD if c == 1 else T
+                width = T + PAD if c < 2 else T
                 windows[c, t] = keep.tile([P, width], F32, name=f"win{c}{t}")
-                if c == 1:
+                if c < 2:
                     nc.gpsimd.memset(windows[c, t][:, T:width], 0.0)
             for h in range(2):
                 w_raw[c, h] = keep.tile([P, 4, PACK, K], F32, name=f"wraw{c}{h}")
@@ -69,7 +69,7 @@ def tile_moe_bdx_lin_none_kernel(tc, dyT, w, gate, offs, out):
         gathered = {}
 
         def new_gathered(c, q, n):
-            gathered[c, q] = stage.tile([P, PACK, n], F32, tag="gathered_b" if (c, q) in ((1, 0), (2, 1)) else "gathered_a", bufs=1 if (c, q) in ((1, 0), (2, 1)) else 2, name=f"gathered{c}{q}")
+            gathered[c, q] = stage.tile([P, PACK, n], F32, tag="gathered", bufs=2, name=f"gathered{c}{q}")
 
         def gather(c, q, t, s0, n):
             nc.vector.tensor_tensor(
@@ -82,7 +82,7 @@ def tile_moe_bdx_lin_none_kernel(tc, dyT, w, gate, offs, out):
         mixed = {}
 
         def new_mixed(c, q, n):
-            mixed[c, q] = stage.tile([P, n, PACK], BF16, align_bytes=64, tag=f"mixed{n}", bufs=1 if n == 1024 else 3, name=f"mixed{c}{q}")
+            mixed[c, q] = stage.tile([P, n, PACK], BF16, align_bytes=64, tag=f"mixed{n}", bufs=2, name=f"mixed{c}{q}")
 
         def mix(dst, src):
             nc.scalar.copy(
@@ -100,7 +100,7 @@ def tile_moe_bdx_lin_none_kernel(tc, dyT, w, gate, offs, out):
         wmixed = {}
 
         def mix_w(c, q):
-            wmixed[c, q] = stage.tile([P, 4, K, PACK], BF16, align_bytes=64, tag="wmix", bufs=6, name=f"wmix{c}{q}")
+            wmixed[c, q] = stage.tile([P, 4, K, PACK], BF16, align_bytes=64, tag="wmix", bufs=4, name=f"wmix{c}{q}")
             nc.scalar.copy(
                 out=wmixed[c, q][:].rearrange("p e (k i) j -> p e k j i", i=RUN),
                 in_=w_raw[c, q][:].rearrange("p e j (k i) -> p e k j i", i=RUN),
@@ -140,104 +140,89 @@ def tile_moe_bdx_lin_none_kernel(tc, dyT, w, gate, offs, out):
 
         nc.sync.dma_start(offsets[:], offs)
         load_window(0, 0)
-        load_gates(0, 512)
-        load_window(0, 1)
-        load_window(0, 2)
-        load_window(0, 3)
-        load_gates(512, 1024)
+        load_gates(0, 256)
+        load_gates(256, 1024)
         for kind, c, i in LOADS:
             (load_window if kind == "y" else load_w)(c, i)
 
-        def g0(q, t):
+        def g01(c, t):
             if t == 0:
-                new_gathered(0, q, 512)
-            gather(0, q, t, 512 * q, 512)
-
-        def g1(t):
-            if t == 0:
-                new_gathered(1, 0, 1024)
-            gather(1, 0, t, 0, 1024)
+                new_gathered(c, 0, S)
+            for s0, n in ((0, 256), (256, 768)) if (c, t) == (0, 0) else ((0, S),):
+                nc.vector.tensor_tensor(
+                    gathered[c, 0][:, t, s0 : s0 + n],
+                    windows[c, t][:].indirect(offsets[:, s0 // 16 : (s0 + n) // 16]),
+                    gates[:, s0 : s0 + n],
+                    MULT,
+                )
 
         def g2(q, t):
             if t == 0:
                 new_gathered(2, q, 512)
             gather(2, q, t, 512 * q, 512)
 
-        def m0(q):
-            new_mixed(0, q, 512)
-            mix(mixed[0, q][:], gathered[0, q][:])
+        def m01(c):
+            new_mixed(c, 0, S)
+            mix(mixed[c, 0][:], gathered[c, 0][:])
 
-        def m1():
-            new_mixed(1, 0, 1024)
-            mix(mixed[1, 0][:], gathered[1, 0][:])
+        def m2(i):
+            n = (512, 256, 256)[i]
+            new_mixed(2, i, n)
+            src = gathered[2, 0][:] if i == 0 else gathered[2, 1][:, :, 256 * i - 256 : 256 * i]
+            mix(mixed[2, i][:], src)
 
-        def m2a():
-            new_mixed(2, 0, 512)
-            mix(mixed[2, 0][:], gathered[2, 0][:])
-
-        def m2b(i):
-            new_mixed(2, 1 + i, 256)
-            mix(mixed[2, 1 + i][:], gathered[2, 1][:, :, 256 * i : 256 * i + 256])
-
+        g01(0, 0)
         mix_w(0, 0)
-        g0(0, 0)
-        g0(0, 1)
-        g0(0, 2)
-        g0(0, 3)
-        g0(1, 0)
-        g0(1, 1)
         mix_w(0, 1)
-        g0(1, 2)
-        m0(0)
-        g0(1, 3)
+        g01(0, 1)
+        g01(0, 2)
+        g01(0, 3)
+        g01(1, 0)
         mix_w(1, 0)
-        g1(0)
-        quant_w(0, 1)
-        g1(1)
-        quant_g(0, 0, 0, 512)
-        g1(2)
-        g1(3)
-        mix_w(1, 1)
+        m01(0)
+        g01(1, 1)
+        g01(1, 2)
+        g01(1, 3)
         g2(0, 0)
+        quant_w(0, 0)
         g2(0, 1)
+        quant_g(0, 0, 0, 1024)
+        multiply(0, 0)
+        multiply(0, 2)
+        mix_w(1, 1)
         mix_w(2, 0)
-        mix_w(2, 1)
-        m1()
-        m0(1)
+        m01(1)
+        g2(0, 2)
         quant_g(1, 0, 0, 1024)
-        quant_w(2, 0)
-        quant_g(0, 1, 512, 512)
+        quant_w(0, 1)
         multiply(0, 4)
         multiply(0, 6)
-        g2(0, 2)
         g2(0, 3)
+        g2(1, 0)
+        g2(1, 1)
+        m2(0)
+        quant_w(1, 0)
+        multiply(1, 0)
+        multiply(1, 2)
+        g2(1, 2)
+        mix_w(2, 1)
+        g2(1, 3)
+        quant_g(2, 0, 0, 512)
         quant_w(1, 1)
         multiply(1, 4)
         multiply(1, 6)
-        m2a()
-        quant_w(1, 0)
-        quant_g(2, 0, 0, 512)
-        quant_w(0, 0)
-        multiply(0, 0)
-        multiply(0, 2)
-        multiply(1, 0)
-        multiply(1, 2)
-        g2(1, 0)
-        finish(0)
-        g2(1, 1)
-        quant_w(2, 1)
-        g2(1, 2)
-        g2(1, 3)
-        m2b(0)
-        finish(1)
+        m2(1)
+        quant_w(2, 0)
         quant_g(2, 1, 512, 256)
+        finish(0)
+        m2(2)
         scatter(0, 256)
+        finish(1)
+        scatter(256, 256)
+        quant_w(2, 1)
         finish(2)
-        m2b(1)
-        scatter(256, 128)
         quant_g(2, 2, 768, 256)
-        finish(3)
-        scatter(384, 128)
         scatter(512, 256)
+        finish(3)
         scatter(768, 256)
         nc.sync.dma_start(out=out, in_=result[:])

from contextlib import ExitStack

import concourse.mybir as mybir

F32 = mybir.dt.float32
BF16 = mybir.dt.bfloat16
U32 = mybir.dt.uint32
U16 = mybir.dt.uint16
U8 = mybir.dt.uint8
FP8X4 = mybir.dt.float8_e4m3fn_x4
MULT = mybir.AluOpType.mult

K, T, E, C, N = 128, 1024, 8, 128, 1536
S = E * C
P = 128
PACK = 4
K_PASS = P * PACK
PASSES = N // K_PASS
PAD = 32
RUN = 4
LOADS = [(x[0], int(x[1]), int(x[2])) for x in "y01 y02 w00 w01 y03 y10 w02 y11 w03 w10 y12 y13 w11 w12 w13 y20 y21 y22 y23 w20 w21 w22 w23".split(" ")]

FLOPS = 2 * K * N * S
BYTES = 4 * (N * T + E * N * K + K * T + S) + 2 * S


def tile_moe_bdx_lin_none_kernel(tc, dyT, w, gate, offs, out):
    nc = tc.nc
    with ExitStack() as ctx:
        keep = ctx.enter_context(tc.tile_pool(name="keep", bufs=1))
        stage = ctx.enter_context(tc.tile_pool(name="stage", bufs=2))
        psum = ctx.enter_context(tc.psum_pool(name="psum", bufs=1))

        offsets = keep.tile([P, S // 16], U16, name="offsets")
        gates = keep.tile([P, S], F32, name="gates")
        windows = {}
        w_raw = {}
        for c in range(PASSES):
            for t in range(PACK):
                width = T + PAD if c < 2 else T
                windows[c, t] = keep.tile([P, width], F32, name=f"win{c}{t}")
                if c < 2:
                    nc.gpsimd.memset(windows[c, t][:, T:width], 0.0)
            for h in range(2):
                w_raw[c, h] = keep.tile([P, 4, PACK, K], F32, name=f"wraw{c}{h}")
        g_codes = keep.tile([P, PASSES, S], U32, align_bytes=64, name="g_codes")
        g_scales = keep.tile([P, PASSES, S], U8, align_bytes=64, name="g_scales")
        w_codes = keep.tile([P, PASSES, E * K], U32, align_bytes=64, name="w_codes")
        w_scales = keep.tile([P, PASSES, E * K], U8, align_bytes=64, name="w_scales")
        result = keep.tile([P, T], F32, name="result")
        slots = keep.tile([P, S], F32, name="slots")
        acc = [psum.tile([P, 2 * C], F32, name=f"acc{b}") for b in range(E // 2)]

        dy_rows = dyT.rearrange("(c p j) t -> c p j t", p=P, j=PACK)
        w_rows = w.rearrange("e (c p j) k -> c p e (j k)", p=P, j=PACK)

        def load_window(c, t):
            nc.sync.dma_start(out=windows[c, t][:, 0:T], in_=dy_rows[c, :, t, :])

        def load_w(c, h):
            nc.sync.dma_start(
                out=w_raw[c, h // 2][:, 2 * (h % 2) : 2 * (h % 2) + 2].rearrange("p e j k -> p e (j k)"),
                in_=w_rows[c, :, 2 * h : 2 * h + 2, :],
            )

        def load_gates(s0, s1):
            nc.sync.dma_start(out=gates[:, s0:s1], in_=gate[0:P, s0:s1])

        gathered = {}

        def new_gathered(c, q, n):
            gathered[c, q] = stage.tile([P, PACK, n], F32, tag="gathered", bufs=2, name=f"gathered{c}{q}")

        def gather(c, q, t, s0, n):
            nc.vector.tensor_tensor(
                gathered[c, q][:, t, :],
                windows[c, t][:].indirect(offsets[:, s0 // 16 : (s0 + n) // 16]),
                gates[:, s0 : s0 + n],
                MULT,
            )

        mixed = {}

        def new_mixed(c, q, n):
            mixed[c, q] = stage.tile([P, n, PACK], BF16, align_bytes=64, tag=f"mixed{n}", bufs=2, name=f"mixed{c}{q}")

        def mix(dst, src):
            nc.scalar.copy(
                out=dst.rearrange("p (n i) t -> p n t i", i=RUN),
                in_=src.rearrange("p t (n i) -> p n t i", i=RUN),
            )

        def quant_g(c, q, s0, n):
            nc.vector.quantize_mx(
                out=g_codes[:, c, s0 : s0 + n].bitcast(FP8X4),
                scales=g_scales[:, c, s0 : s0 + n],
                in_=mixed[c, q][:].rearrange("p n t -> p (n t)"),
            )

        wmixed = {}

        def mix_w(c, q):
            wmixed[c, q] = stage.tile([P, 4, K, PACK], BF16, align_bytes=64, tag="wmix", bufs=4, name=f"wmix{c}{q}")
            nc.scalar.copy(
                out=wmixed[c, q][:].rearrange("p e (k i) j -> p e k j i", i=RUN),
                in_=w_raw[c, q][:].rearrange("p e j (k i) -> p e k j i", i=RUN),
            )

        def quant_w(c, q):
            cols = slice(q * 4 * K, (q + 1) * 4 * K)
            nc.vector.quantize_mx(
                out=w_codes[:, c, cols].bitcast(FP8X4),
                scales=w_scales[:, c, cols],
                in_=wmixed[c, q][:].rearrange("p e k j -> p (e k j)"),
            )

        def multiply(c, e):
            cols = slice(e * C, (e + 1) * C)
            half = (e % 2) * C
            nc.tensor.matmul_mx(
                out=acc[e // 2][:, half : half + C],
                lhsT=w_codes[:, c, cols].bitcast(FP8X4),
                lhsT_scale=w_scales[:, c, cols],
                rhs=g_codes[:, c, cols].bitcast(FP8X4),
                rhs_scale=g_scales[:, c, cols],
                start=(c == 0),
                stop=(c == PASSES - 1),
            )

        def finish(b):
            multiply(2, 2 * b)
            for c in range(PASSES):
                multiply(c, 2 * b + 1)
            nc.scalar.copy(out=slots[:, 2 * b * C : 2 * (b + 1) * C], in_=acc[b][:])

        def scatter(s0, n):
            nc.vector.tensor_copy(
                out=result[:].indirect(offsets[:, s0 // 16 : (s0 + n) // 16]), in_=slots[:, s0 : s0 + n]
            )

        nc.sync.dma_start(offsets[:], offs)
        load_window(0, 0)
        load_gates(0, 256)
        load_gates(256, 1024)
        for kind, c, i in LOADS:
            (load_window if kind == "y" else load_w)(c, i)

        def g01(c, t):
            if t == 0:
                new_gathered(c, 0, S)
            for s0, n in ((0, 256), (256, 768)) if (c, t) == (0, 0) else ((0, S),):
                nc.vector.tensor_tensor(
                    gathered[c, 0][:, t, s0 : s0 + n],
                    windows[c, t][:].indirect(offsets[:, s0 // 16 : (s0 + n) // 16]),
                    gates[:, s0 : s0 + n],
                    MULT,
                )

        def g2(q, t):
            if t == 0:
                new_gathered(2, q, 512)
            gather(2, q, t, 512 * q, 512)

        def m01(c):
            new_mixed(c, 0, S)
            mix(mixed[c, 0][:], gathered[c, 0][:])

        def m2(i):
            n = (512, 256, 256)[i]
            new_mixed(2, i, n)
            src = gathered[2, 0][:] if i == 0 else gathered[2, 1][:, :, 256 * i - 256 : 256 * i]
            mix(mixed[2, i][:], src)

        g01(0, 0)
        mix_w(0, 0)
        mix_w(0, 1)
        g01(0, 1)
        g01(0, 2)
        g01(0, 3)
        g01(1, 0)
        mix_w(1, 0)
        m01(0)
        g01(1, 1)
        g01(1, 2)
        g01(1, 3)
        g2(0, 0)
        quant_w(0, 0)
        g2(0, 1)
        quant_g(0, 0, 0, 1024)
        multiply(0, 0)
        multiply(0, 2)
        mix_w(1, 1)
        mix_w(2, 0)
        m01(1)
        g2(0, 2)
        quant_g(1, 0, 0, 1024)
        quant_w(0, 1)
        multiply(0, 4)
        multiply(0, 6)
        g2(0, 3)
        g2(1, 0)
        g2(1, 1)
        m2(0)
        quant_w(1, 0)
        multiply(1, 0)
        multiply(1, 2)
        g2(1, 2)
        mix_w(2, 1)
        g2(1, 3)
        quant_g(2, 0, 0, 512)
        quant_w(1, 1)
        multiply(1, 4)
        multiply(1, 6)
        m2(1)
        quant_w(2, 0)
        quant_g(2, 1, 512, 256)
        finish(0)
        m2(2)
        scatter(0, 256)
        finish(1)
        scatter(256, 256)
        quant_w(2, 1)
        finish(2)
        quant_g(2, 2, 768, 256)
        scatter(512, 256)
        finish(3)
        scatter(768, 256)
        nc.sync.dma_start(out=out, in_=result[:])
